import numpy as np
import ml_dtypes


def mxq(x, axis, fmt="e4m3"):
    dtype, down = {"e4m3": (ml_dtypes.float8_e4m3fn, 7), "e5m2": (ml_dtypes.float8_e5m2, 14)}[fmt]
    v = np.moveaxis(np.asarray(x, np.float32).astype(ml_dtypes.bfloat16).astype(np.float64), axis, -1)
    blocks = v.reshape(v.shape[:-1] + (-1, 32))
    amax = np.abs(blocks).max(-1, keepdims=True)
    byte = np.maximum(np.where(amax > 0, np.frexp(amax)[1] - 1 + 127, 0) - down, 1)
    scale = np.exp2(byte - 127.0)
    codes = (blocks / scale).astype(np.float32).astype(dtype).astype(np.float64)
    return np.moveaxis((codes * scale).reshape(v.shape), -1, axis)


WIDE = False


def mx_kscale(k):
    if not WIDE:
        return np.ones(k)
    levels = np.array([30, -30])
    if k % 512:
        return np.exp2(np.random.permutation(np.resize(levels, k // 32))).repeat(32)
    a = np.empty((k // 512, 16))
    for p in range(k // 512):
        a[p, :8] = np.random.permutation(np.resize(levels, 8))
        for g in range(8):
            far = levels[np.abs(levels - a[p, g]) >= 10]
            a[p, g + 8] = far[np.random.randint(len(far))]
    return np.exp2(a.ravel()).repeat(32)


def f64(x):
    return np.asarray(x).astype(np.float64)


def striped(idx):
    return np.tile(np.asarray(idx).reshape(-1, 16).T, (8, 1)).astype(np.uint16)


def unstriped(offs):
    return offs[:16].T.reshape(-1).astype(np.int64)


def striped8(idx):
    return np.asarray(idx).reshape(8, -1, 16).transpose(0, 2, 1).reshape(128, -1).astype(np.uint16)


def unstriped8(offs):
    return offs.reshape(8, 16, -1).transpose(0, 2, 1).reshape(8, -1).astype(np.int64)


def pick8(x, idx, run):
    r = np.arange(len(x))
    return x[r[:, None], idx[r % (8 * run) // run]]


E2M1 = np.array([0.0, 0.5, 1.0, 1.5, 2.0, 3.0, 4.0, 6.0, -0.0, -0.5, -1.0, -1.5, -2.0, -3.0, -4.0, -6.0])


def pack_weight(w, fmt):
    k, n = w.shape
    w = f64(np.asarray(w, np.float32).astype(ml_dtypes.bfloat16)).reshape(k // 32, 32, n)
    amax = np.abs(w).max(1)
    if fmt in ("e4m3", "e5m2"):
        byte = np.frexp(amax)[1] - 1 + 127 - (7 if fmt == "e4m3" else 14)
    else:
        mant, ex = np.frexp(amax / 6.0)
        byte = np.where(mant > 0.5, ex, ex - 1) + 127
    byte = np.clip(np.where(amax > 0, byte, 1), 1, 254)
    scaled = (w * np.exp2(127.0 - byte)[:, None, :]).reshape(k, n).astype(np.float32)
    by_word = np.ascontiguousarray(scaled.reshape(k // 512, 128, 4, n).transpose(0, 1, 3, 2))
    if fmt in ("e4m3", "e5m2"):
        words = by_word.astype(ml_dtypes.float8_e4m3fn if fmt == "e4m3" else ml_dtypes.float8_e5m2).view(np.uint8)
    else:
        c = by_word.astype(ml_dtypes.float4_e2m1fn).view(np.uint8) & 0xF
        words = (c[..., 0::2] | (c[..., 1::2] << 4)).reshape(k // 512, 128, 2 * n)
    return np.ascontiguousarray(words), np.ascontiguousarray(byte.astype(np.uint8).reshape(k // 512, 16, n))


def unpack_weight(words, scales, fmt):
    g, _, n = scales.shape
    words = np.ascontiguousarray(words).reshape(g, 128, n, -1)
    if fmt in ("e4m3", "e5m2"):
        vals = words.view(ml_dtypes.float8_e4m3fn if fmt == "e4m3" else ml_dtypes.float8_e5m2).astype(np.float64)
    else:
        nib = np.empty((g, 128, n, 4), np.uint8)
        nib[..., 0::2] = words & 0xF
        nib[..., 1::2] = words >> 4
        vals = E2M1[nib]
    vals = vals * np.repeat(np.exp2(scales.astype(np.float64) - 127.0), 8, axis=1)[..., None]
    return vals.transpose(0, 1, 3, 2).reshape(g * 512, n)


K, T, J, R, F, Z, C, O, N, E = 512, 1024, 256, 512, 512, 1024, 512, 128, 256, 512


def setup_inputs():
    n = np.random.standard_normal
    idx = np.random.permutation(T)[:J]
    idx2 = np.random.permutation(Z)[:J]
    idx3 = np.stack([np.random.permutation(C)[:J] for _ in range(8)])
    idx4 = np.random.permutation(C)[:O]
    idx5 = np.random.permutation(C)[:O]
    idx6 = np.random.permutation(J)[:O]
    idx7 = np.stack([np.random.permutation(E)[:O] for _ in range(8)])
    fk = mx_kscale(K)
    ff = mx_kscale(F)
    fr = mx_kscale(R)
    xtp = pack_weight(n((K, T)) / fk[:, None], "e4m3")
    xop = pack_weight(n((F, Z)) / ff[:, None], "e2m1")
    wp = pack_weight(n((K, R)) * 1 / np.sqrt(K) * fk[:, None] * fr, "e2m1")
    w0p = pack_weight(n((F, R)) * 1 / np.sqrt(F) * ff[:, None] * fr, "e5m2")
    w2p = pack_weight(n((F, R)) * 1 / np.sqrt(F) * ff[:, None] * fr, "e5m2")
    wbp = pack_weight(n((R, N)) * 1 / np.sqrt(R) / fr[:, None], "e5m2")
    return {
        "xt_words": xtp[0],
        "xt_scales": xtp[1],
        "xo_words": xop[0],
        "xo_scales": xop[1],
        "w_words": wp[0],
        "w_scales": wp[1],
        "w0_words": w0p[0],
        "w0_scales": w0p[1],
        "w2_words": w2p[0],
        "w2_scales": w2p[1],
        "sa": (np.random.uniform(0.5, 1.6, (R, 1))).astype(np.float32),
        "sb": (np.random.uniform(0.5, 1.6, (R, 1))).astype(np.float32),
        "sd": (np.random.uniform(0.5, 1.6, (R, 1))).astype(np.float32),
        "wb_words": wbp[0],
        "wb_scales": wbp[1],
        "offs": striped(idx),
        "offs2": striped(idx2),
        "offs3": striped8(idx3),
        "offs4": striped(idx4),
        "offs5": striped(idx5),
        "offs6": striped(idx6),
        "offs7": striped8(idx7),
    }


def reference(xt_words, xt_scales, xo_words, xo_scales, w_words, w_scales, w0_words, w0_scales, w2_words, w2_scales, sa, sb, sd, wb_words, wb_scales, offs, offs2, offs3, offs4, offs5, offs6, offs7):
    idx = unstriped(offs)
    idx2 = unstriped(offs2)
    idx3 = unstriped8(offs3)
    idx4 = unstriped(offs4)
    idx5 = unstriped(offs5)
    idx6 = unstriped(offs6)
    idx7 = unstriped8(offs7)
    xtu = unpack_weight(xt_words, xt_scales, "e4m3")
    xou = unpack_weight(xo_words, xo_scales, "e2m1")
    wu = unpack_weight(w_words, w_scales, "e2m1")
    w0u = unpack_weight(w0_words, w0_scales, "e5m2")
    w2u = unpack_weight(w2_words, w2_scales, "e5m2")
    wbu = unpack_weight(wb_words, wb_scales, "e5m2")
    xtidxg = xtu[:, idx]
    xoidx2g = xou[:, idx2]
    a = wu.T @ xtidxg + w0u.T @ xoidx2g
    b = w2u.T @ xoidx2g
    pw = np.zeros((R, C))
    pw[np.arange(R)[:, None], idx3[np.arange(R) % 512 // 64]] = a
    hid = np.maximum(pw[:, idx4] * f64(sa), pw[:, idx5] * f64(sb)) - b[:, idx6] * f64(sd)
    hidq = mxq(hid, 0, "e4m3")
    p = wbu.T @ hidq
    y = np.zeros((N, E))
    y[np.arange(N)[:, None], idx7[np.arange(N) % 128 // 16]] = p
    return y

@@ -1,0 +1,203 @@
+from contextlib import ExitStack
+
+import concourse.mybir as mybir
+
+F32 = mybir.dt.float32
+BF16 = mybir.dt.bfloat16
+I32 = mybir.dt.int32
+U32 = mybir.dt.uint32
+U16 = mybir.dt.uint16
+U8 = mybir.dt.uint8
+E4M3 = mybir.dt.float8_e4m3fn_x4
+E5M2 = mybir.dt.float8_e5m2_x4
+E2M1 = mybir.dt.float4_e2m1fn_x4
+COPY = mybir.ActivationFunctionType.Copy
+ALU = mybir.AluOpType
+
+P = 128
+PACK = 4
+K, T, J, R, F, Z, C, O, N, E = 512, 1024, 256, 512, 512, 1024, 512, 128, 256, 512
+FLOPS = 2 * (K * R * J + 2 * F * R * J + R * N * O)
+
+
+def tile_list_ownthree_noted_one_ownpage_kernel(
+    tc, xt_words, xt_scales, xo_words, xo_scales, w_words, w_scales, w0_words, w0_scales,
+    w2_words, w2_scales, sa, sb, sd, wb_words, wb_scales,
+    offs, offs2, offs3, offs4, offs5, offs6, offs7, out,
+):
+    nc = tc.nc
+    with ExitStack() as ctx:
+        keep = ctx.enter_context(tc.tile_pool(name="keep", bufs=1))
+        psum = ctx.enter_context(tc.psum_pool(name="psum", bufs=1))
+
+        def sbuf(name, shape, dtype, tag=None):
+            return keep.tile(shape, dtype, name=name, tag=tag or name, align_bytes=64)
+
+        def load_list(name, src):
+            tile = keep.tile(list(src.shape), U16, name=name)
+            nc.sync.dma_start(tile[:], src)
+            return tile
+
+        def load_words(name, src, columns, dtype):
+            tile = sbuf(name, [P, columns], dtype)
+            rows = src[0] if len(src.shape) == 3 else src[0].rearrange("p n t -> p (n t)")
+            nc.sync.dma_start(tile[:].bitcast(I32), rows.bitcast(I32))
+            return tile
+
+        def load_scale_rows(stage, src, first):
+            words = src.shape[2] // 4
+            rows = src[0].bitcast(I32).rearrange("(s q r) n -> q r s n", s=2, q=2)
+            for q in range(2):
+                nc.sync.dma_start(stage[32 * q : 32 * q + 4, :, first : first + words], rows[q])
+
+        def load_factor(name, src):
+            tile = sbuf(name, [P, PACK], F32)
+            nc.sync.dma_start(tile[:], src.rearrange("(p t) o -> p (t o)", t=PACK))
+            return tile
+
+        def dealt(dst, src, run):
+            return (
+                dst.rearrange("p (t c i) -> p c t i", t=PACK, i=run),
+                src.rearrange("p (c i t) -> p c t i", t=PACK, i=run),
+            )
+
+        xo_stage = sbuf("xo_stage", [64, 2, Z // 4], I32)
+        xt_stage = sbuf("xt_stage", [64, 2, T // 4], I32)
+        a_stage = sbuf("a_stage", [P, 2, 2 * R // 4], I32)
+        b_stage = sbuf("b_stage", [P, 2, (R + N) // 4], I32)
+        nc.vector.memset(xo_stage[:], 0)
+        nc.vector.memset(xt_stage[:], 0)
+        nc.vector.memset(a_stage[0:64], 0)
+        nc.vector.memset(b_stage[0:64], 0)
+
+        load_scale_rows(xo_stage, xo_scales, 0)
+        list2 = load_list("list2", offs2)
+        xo_w = load_words("xo_w", xo_words, Z, U16)
+        load_scale_rows(xt_stage, xt_scales, 0)
+        list1 = load_list("list1", offs)
+        xt_w = load_words("xt_w", xt_words, T, U32)
+        load_scale_rows(a_stage, w0_scales, 0)
+        w0_w = load_words("w0_w", w0_words, R, U32)
+        load_scale_rows(a_stage, w_scales, R // 4)
+        w_w = load_words("w_w", w_words, R, U16)
+        list3 = load_list("list3", offs3)
+        load_scale_rows(b_stage, w2_scales, 0)
+        load_scale_rows(b_stage, wb_scales, R // 4)
+        w2_w = load_words("w2_w", w2_words, R, I32)
+        wb_w = load_words("wb_w", wb_words, N, U32)
+        list7 = load_list("list7", offs7)
+        list4 = load_list("list4", offs4)
+        sa_t = load_factor("sa_t", sa)
+        list5 = load_list("list5", offs5)
+        sb_t = load_factor("sb_t", sb)
+        list6 = load_list("list6", offs6)
+        sd_t = load_factor("sd_t", sd)
+
+        boards = [sbuf(f"board{i}", [P, C], F32) for i in range(2)]
+        for tile in boards:
+            nc.vector.memset(tile[:], 0.0)
+
+        def gather_scales(name, stage, columns, offsets):
+            plane = sbuf(name + "_plane", [P, columns], U8)
+            for s in range(2):
+                nc.vector.tensor_copy(plane[64 * s : 64 * s + 64, :].bitcast(I32), stage[:, s, :])
+            picked = sbuf(name + "_picked", [P, J], U8)
+            nc.vector.tensor_copy(picked[:], plane[:].indirect(offsets[:]))
+            return picked
+
+        def gather_words(name, words, dtype, offsets):
+            picked = sbuf(name, [P, J], dtype)
+            nc.vector.tensor_copy(picked[:], words[:].indirect(offsets[:]))
+            return picked
+
+        xo_gs = gather_scales("xo_s", xo_stage, Z, list2)
+        xo_gw = gather_words("xo_gw", xo_w, U16, list2)
+        xt_gs = gather_scales("xt_s", xt_stage, T, list1)
+
+        nc.vector.tensor_copy(a_stage[64:128, 0, :], a_stage[0:64, 1, :])
+        w0_s = sbuf("w0_s", [P, R], U8)
+        w_s = sbuf("w_s", [P, R], U8)
+        a_plane = a_stage[:, 0, :].bitcast(U8)
+        nc.vector.tensor_copy(*dealt(w0_s[:], a_plane[:, 0:R], 16))
+        nc.vector.tensor_copy(*dealt(w_s[:], a_plane[:, R : 2 * R], 16))
+        w0_d = sbuf("w0_d", [P, R], U32)
+        w_d = sbuf("w_d", [P, R], U16)
+        nc.scalar.copy(*dealt(w0_d[:], w0_w[:], 4))
+        nc.scalar.copy(*dealt(w_d[:], w_w[:], 8))
+        xt_gw = gather_words("xt_gw", xt_w, U32, list1)
+
+        boards.append(sbuf("board2", [P, C], F32, tag="xt_w"))
+        nc.gpsimd.memset(boards[2][:], 0.0)
+
+        a_banks = [psum.tile([P, J], F32, name=f"a_bank{t}") for t in range(PACK)]
+        for t in range(PACK):
+            cols = slice(P * t, P * (t + 1))
+            nc.tensor.matmul_mx(a_banks[t][:], lhsT=w0_d[:, cols].bitcast(E5M2), lhsT_scale=w0_s[:, cols],
+                                rhs=xo_gw[:].bitcast(E2M1), rhs_scale=xo_gs[:], start=True, stop=False)
+        a_rows = []
+        for t in range(PACK):
+            cols = slice(P * t, P * (t + 1))
+            nc.tensor.matmul_mx(a_banks[t][:], lhsT=w_d[:, cols].bitcast(E2M1), lhsT_scale=w_s[:, cols],
+                                rhs=xt_gw[:].bitcast(E4M3), rhs_scale=xt_gs[:], start=False, stop=True)
+            a_t = sbuf(f"a_rows{t}", [P, J], F32)
+            nc.vector.tensor_copy(a_t[:], a_banks[t][:])
+            a_rows.append(a_t)
+
+        nc.vector.tensor_copy(b_stage[64:128, 0, :], b_stage[0:64, 1, :])
+        b_plane = b_stage[:, 0, :].bitcast(U8)
+        w2_s = sbuf("w2_s", [P, R], U8)
+        nc.vector.tensor_copy(*dealt(w2_s[:], b_plane[:, 0:R], 16))
+        w2_d = sbuf("w2_d", [P, R], I32)
+        nc.vector.tensor_copy(*dealt(w2_d[:], w2_w[:], 4))
+        b_banks = [psum.tile([P, 2, J], F32, name=f"b_bank{i}") for i in range(2)]
+        b_rows = []
+        for t in range(PACK):
+            cols = slice(P * t, P * (t + 1))
+            nc.tensor.matmul_mx(b_banks[t // 2][:, t % 2, :], lhsT=w2_d[:, cols].bitcast(E5M2), lhsT_scale=w2_s[:, cols],
+                                rhs=xo_gw[:].bitcast(E2M1), rhs_scale=xo_gs[:], start=True, stop=True)
+        for t in range(PACK):
+            b_t = sbuf(f"b_rows{t}", [P, J], F32)
+            nc.vector.tensor_copy(b_t[:], b_banks[t // 2][:, t % 2, :])
+            b_rows.append(b_t)
+
+        pages = [sbuf(f"page{i}", [P, E], F32, tag=tag) for i, tag in enumerate(("w0_d", "w2_d"))]
+        for tile in pages:
+            nc.gpsimd.memset(tile[:], 0.0)
+
+        hid = sbuf("hid", [P, O, PACK], BF16)
+
+        def put(t):
+            nc.scalar.activation(boards[t % 3][:].indirect(list3[:]), a_rows[t][:], COPY)
+
+        def join(t):
+            first = sbuf(f"first{t}", [P, O], F32)
+            second = sbuf(f"second{t}", [P, O], F32)
+            third = sbuf(f"third{t}", [P, O], F32)
+            larger = sbuf(f"larger{t}", [P, O], F32)
+            board = boards[t % 3]
+            nc.scalar.activation(first[:], board[:].indirect(list4[:]), COPY, scale=sa_t[:, t : t + 1])
+            nc.scalar.activation(second[:], board[:].indirect(list5[:]), COPY, scale=sb_t[:, t : t + 1])
+            nc.scalar.activation(third[:], b_rows[t][:].indirect(list6[:]), COPY, scale=sd_t[:, t : t + 1])
+            nc.vector.tensor_tensor(larger[:], first[:], second[:], ALU.max)
+            nc.vector.tensor_tensor(hid[:, :, t], larger[:], third[:], ALU.subtract)
+
+        for t in range(3):
+            put(t)
+        join(0)
+        put(3)
+        for t in range(1, PACK):
+            join(t)
+
+        hid_w = sbuf("hid_w", [P, O], U32)
+        hid_s = sbuf("hid_s", [P, O], U8)
+        nc.vector.quantize_mx(out=hid_w[:].bitcast(E4M3), scales=hid_s[:], in_=hid[:].rearrange("p o t -> p (o t)"))
+
+        for i in range(N // P):
+            p_bank = psum.tile([P, O], F32, name=f"p_bank{i}")
+            nc.tensor.matmul_mx(p_bank[:], lhsT=wb_w[:, P * i : P * (i + 1)].bitcast(E5M2),
+                                lhsT_scale=b_plane[:, R + P * i : R + P * (i + 1)],
+                                rhs=hid_w[:].bitcast(E4M3), rhs_scale=hid_s[:], start=True, stop=True)
+            p_rows = sbuf(f"p_rows{i}", [P, O], F32)
+            nc.vector.tensor_copy(p_rows[:], p_bank[:])
+            nc.scalar.activation(pages[i][:].indirect(list7[:]), p_rows[:], COPY)
+            nc.sync.dma_start(out[P * i : P * (i + 1), :], pages[i][:])

@@ -30,18 +30,23 @@ def tile_list_ownthree_noted_one_ownpage_kernel(
         keep = ctx.enter_context(tc.tile_pool(name="keep", bufs=1))
         psum = ctx.enter_context(tc.psum_pool(name="psum", bufs=1))
 
+        reuse = ctx.enter_context(tc.tile_pool(name="reuse", bufs=1))
+
         def sbuf(name, shape, dtype, tag=None):
             return keep.tile(shape, dtype, name=name, tag=tag or name, align_bytes=64)
+
+        def placed(name, shape, dtype, offset):
+            return reuse.tile(shape, dtype, name=name, offset=offset, align_bytes=64)
 
         def load_list(name, src):
             tile = keep.tile(list(src.shape), U16, name=name)
             nc.sync.dma_start(tile[:], src)
             return tile
 
-        def load_words(name, src, columns, dtype):
+        def load_words(name, src, columns, dtype, queue=nc.sync):
             tile = sbuf(name, [P, columns], dtype)
             rows = src[0] if len(src.shape) == 3 else src[0].rearrange("p n t -> p (n t)")
-            nc.sync.dma_start(tile[:].bitcast(I32), rows.bitcast(I32))
+            queue.dma_start(tile[:].bitcast(I32), rows.bitcast(I32))
             return tile
 
         def load_scale_rows(stage, src, first):
@@ -70,16 +75,16 @@ def tile_list_ownthree_noted_one_ownpage_kernel(
         nc.vector.memset(a_stage[0:64], 0)
         nc.vector.memset(b_stage[0:64], 0)
 
-        load_scale_rows(xo_stage, xo_scales, 0)
         list2 = load_list("list2", offs2)
         xo_w = load_words("xo_w", xo_words, Z, U16)
+        load_scale_rows(xo_stage, xo_scales, 0)
         load_scale_rows(xt_stage, xt_scales, 0)
         list1 = load_list("list1", offs)
         xt_w = load_words("xt_w", xt_words, T, U32)
         load_scale_rows(a_stage, w0_scales, 0)
-        w0_w = load_words("w0_w", w0_words, R, U32)
         load_scale_rows(a_stage, w_scales, R // 4)
-        w_w = load_words("w_w", w_words, R, U16)
+        w0_w = load_words("w0_w", w0_words, R, U32, nc.gpsimd)
+        w_w = load_words("w_w", w_words, R, U16, nc.gpsimd)
         list3 = load_list("list3", offs3)
         load_scale_rows(b_stage, w2_scales, 0)
         load_scale_rows(b_stage, wb_scales, R // 4)
@@ -93,55 +98,67 @@ def tile_list_ownthree_noted_one_ownpage_kernel(
         list6 = load_list("list6", offs6)
         sd_t = load_factor("sd_t", sd)
 
-        boards = [sbuf(f"board{i}", [P, C], F32) for i in range(2)]
-        for tile in boards:
-            nc.vector.memset(tile[:], 0.0)
+        boards = [sbuf(f"board{i}", [P, C], F32) for i in range(PACK)]
+        for i, tile in enumerate(boards):
+            (nc.vector if i < 2 else nc.gpsimd).memset(tile[:], 0.0)
 
-        def gather_scales(name, stage, columns, offsets):
-            plane = sbuf(name + "_plane", [P, columns], U8)
+        def spread(name, stage, columns):
+            plane = sbuf(name, [P, columns], U8)
             for s in range(2):
                 nc.vector.tensor_copy(plane[64 * s : 64 * s + 64, :].bitcast(I32), stage[:, s, :])
-            picked = sbuf(name + "_picked", [P, J], U8)
-            nc.vector.tensor_copy(picked[:], plane[:].indirect(offsets[:]))
+            return plane
+
+        def half(offsets, h):
+            return offsets[:, 8 * h : 8 * h + 8]
+
+        def gather(picked, window, offsets, h):
+            nc.vector.tensor_copy(picked[:], window[:].indirect(half(offsets, h)))
             return picked
 
-        def gather_words(name, words, dtype, offsets):
-            picked = sbuf(name, [P, J], dtype)
-            nc.vector.tensor_copy(picked[:], words[:].indirect(offsets[:]))
-            return picked
-
-        xo_gs = gather_scales("xo_s", xo_stage, Z, list2)
-        xo_gw = gather_words("xo_gw", xo_w, U16, list2)
-        xt_gs = gather_scales("xt_s", xt_stage, T, list1)
-
+        H = J // 2
+        xo_gw = [gather(sbuf("xo_gw0", [P, H], U16), xo_w, list2, 0)]
+        xo_plane = spread("xo_plane", xo_stage, Z)
+        xt_plane = spread("xt_plane", xt_stage, T)
+        xo_gs = [gather(sbuf("xo_gs0", [P, H], U8), xo_plane, list2, 0)]
+        xt_gs = [gather(placed("xt_gs0", [P, H], U8, 512), xt_plane, list1, 0)]
         nc.vector.tensor_copy(a_stage[64:128, 0, :], a_stage[0:64, 1, :])
-        w0_s = sbuf("w0_s", [P, R], U8)
-        w_s = sbuf("w_s", [P, R], U8)
-        a_plane = a_stage[:, 0, :].bitcast(U8)
-        nc.vector.tensor_copy(*dealt(w0_s[:], a_plane[:, 0:R], 16))
-        nc.vector.tensor_copy(*dealt(w_s[:], a_plane[:, R : 2 * R], 16))
-        w0_d = sbuf("w0_d", [P, R], U32)
-        w_d = sbuf("w_d", [P, R], U16)
-        nc.scalar.copy(*dealt(w0_d[:], w0_w[:], 4))
-        nc.scalar.copy(*dealt(w_d[:], w_w[:], 8))
-        xt_gw = gather_words("xt_gw", xt_w, U32, list1)
+        xt_gw = [gather(placed("xt_gw0", [P, H], U32, 0), xt_w, list1, 0)]
+        a_plane = a_stage[:, 0, :].bitcast(U8).rearrange("p (w m t) -> p t w m", w=2, t=PACK)
 
-        boards.append(sbuf("board2", [P, C], F32, tag="xt_w"))
-        nc.gpsimd.memset(boards[2][:], 0.0)
+        w0_dealt = sbuf("w0_dealt", [P, R], U32)
+        w_dealt = sbuf("w_dealt", [P, R], U16)
+        nc.scalar.copy(*dealt(w0_dealt[:], w0_w[:], 4))
+        nc.scalar.copy(*dealt(w_dealt[:], w_w[:], 8))
+        w0_d = [w0_dealt[:, P * t : P * (t + 1)] for t in range(PACK)]
+        w_d = [w_dealt[:, P * t : P * (t + 1)] for t in range(PACK)]
 
-        a_banks = [psum.tile([P, J], F32, name=f"a_bank{t}") for t in range(PACK)]
+        a_banks = [psum.tile([P, 2, H], F32, name=f"a_bank{t}") for t in range(PACK)]
+        a_s = []
+        a_rows = {}
+
+        def first_stage(t, h):
+            nc.tensor.matmul_mx(a_banks[t][:, h, :], lhsT=w0_d[t].bitcast(E5M2), lhsT_scale=a_s[t][:, 0, :],
+                                rhs=xo_gw[h][:].bitcast(E2M1), rhs_scale=xo_gs[h][:], start=True, stop=False)
+            nc.tensor.matmul_mx(a_banks[t][:, h, :], lhsT=w_d[t].bitcast(E2M1), lhsT_scale=a_s[t][:, 1, :],
+                                rhs=xt_gw[h][:].bitcast(E4M3), rhs_scale=xt_gs[h][:], start=False, stop=True)
+            a_rows[t, h] = sbuf(f"a_rows{t}{h}", [P, H], F32)
+            nc.vector.tensor_copy(a_rows[t, h][:], a_banks[t][:, h, :])
+
+        def put(t, h):
+            nc.scalar.activation(boards[t][:].indirect(half(list3, h)), a_rows[t, h][:], COPY)
+
         for t in range(PACK):
-            cols = slice(P * t, P * (t + 1))
-            nc.tensor.matmul_mx(a_banks[t][:], lhsT=w0_d[:, cols].bitcast(E5M2), lhsT_scale=w0_s[:, cols],
-                                rhs=xo_gw[:].bitcast(E2M1), rhs_scale=xo_gs[:], start=True, stop=False)
-        a_rows = []
+            a_s.append(sbuf(f"a_s{t}", [P, 2, P], U8))
+            nc.vector.tensor_copy(a_s[t][:], a_plane[:, t])
+            first_stage(t, 0)
+            put(t, 0)
+
+        xo_gw.append(gather(placed("xo_gw1", [P, H], U16, 0), xo_w, list2, 1))
+        xo_gs.append(gather(placed("xo_gs1", [P, H], U8, 256), xo_plane, list2, 1))
+        xt_gs.append(gather(placed("xt_gs1", [P, H], U8, 384), xt_plane, list1, 1))
+        xt_gw.append(gather(placed("xt_gw1", [P, H], U32, 512), xt_w, list1, 1))
         for t in range(PACK):
-            cols = slice(P * t, P * (t + 1))
-            nc.tensor.matmul_mx(a_banks[t][:], lhsT=w_d[:, cols].bitcast(E2M1), lhsT_scale=w_s[:, cols],
-                                rhs=xt_gw[:].bitcast(E4M3), rhs_scale=xt_gs[:], start=False, stop=True)
-            a_t = sbuf(f"a_rows{t}", [P, J], F32)
-            nc.vector.tensor_copy(a_t[:], a_banks[t][:])
-            a_rows.append(a_t)
+            first_stage(t, 1)
 
         nc.vector.tensor_copy(b_stage[64:128, 0, :], b_stage[0:64, 1, :])
         b_plane = b_stage[:, 0, :].bitcast(U8)
@@ -149,44 +166,47 @@ def tile_list_ownthree_noted_one_ownpage_kernel(
         nc.vector.tensor_copy(*dealt(w2_s[:], b_plane[:, 0:R], 16))
         w2_d = sbuf("w2_d", [P, R], I32)
         nc.vector.tensor_copy(*dealt(w2_d[:], w2_w[:], 4))
-        b_banks = [psum.tile([P, 2, J], F32, name=f"b_bank{i}") for i in range(2)]
+        b_banks = [psum.tile([P, 2, 2, H], F32, name=f"b_bank{i}") for i in range(2)]
         b_rows = []
         for t in range(PACK):
             cols = slice(P * t, P * (t + 1))
-            nc.tensor.matmul_mx(b_banks[t // 2][:, t % 2, :], lhsT=w2_d[:, cols].bitcast(E5M2), lhsT_scale=w2_s[:, cols],
-                                rhs=xo_gw[:].bitcast(E2M1), rhs_scale=xo_gs[:], start=True, stop=True)
+            for h in range(2):
+                nc.tensor.matmul_mx(b_banks[t // 2][:, t % 2, h, :], lhsT=w2_d[:, cols].bitcast(E5M2), lhsT_scale=w2_s[:, cols],
+                                    rhs=xo_gw[h][:].bitcast(E2M1), rhs_scale=xo_gs[h][:], start=True, stop=True)
         for t in range(PACK):
             b_t = sbuf(f"b_rows{t}", [P, J], F32)
-            nc.vector.tensor_copy(b_t[:], b_banks[t // 2][:, t % 2, :])
+            nc.vector.tensor_copy(b_t[:], b_banks[t // 2][:, t % 2].rearrange("p h j -> p (h j)"))
             b_rows.append(b_t)
 
-        pages = [sbuf(f"page{i}", [P, E], F32, tag=tag) for i, tag in enumerate(("w0_d", "w2_d"))]
+        pages = [sbuf(f"page{i}", [P, E], F32, tag=tag) for i, tag in enumerate(("xt_w", "xo_w"))]
         for tile in pages:
             nc.gpsimd.memset(tile[:], 0.0)
 
         hid = sbuf("hid", [P, O, PACK], BF16)
 
-        def put(t):
-            nc.scalar.activation(boards[t % 3][:].indirect(list3[:]), a_rows[t][:], COPY)
+        larger = {}
 
-        def join(t):
+        def pick(t):
             first = sbuf(f"first{t}", [P, O], F32)
             second = sbuf(f"second{t}", [P, O], F32)
-            third = sbuf(f"third{t}", [P, O], F32)
-            larger = sbuf(f"larger{t}", [P, O], F32)
-            board = boards[t % 3]
-            nc.scalar.activation(first[:], board[:].indirect(list4[:]), COPY, scale=sa_t[:, t : t + 1])
-            nc.scalar.activation(second[:], board[:].indirect(list5[:]), COPY, scale=sb_t[:, t : t + 1])
-            nc.scalar.activation(third[:], b_rows[t][:].indirect(list6[:]), COPY, scale=sd_t[:, t : t + 1])
-            nc.vector.tensor_tensor(larger[:], first[:], second[:], ALU.max)
-            nc.vector.tensor_tensor(hid[:, :, t], larger[:], third[:], ALU.subtract)
+            larger[t] = sbuf(f"larger{t}", [P, O], F32, tag="w2_d" if t == 0 else None)
+            nc.scalar.activation(first[:], boards[t][:].indirect(list4[:]), COPY, scale=sa_t[:, t : t + 1])
+            nc.scalar.activation(second[:], boards[t][:].indirect(list5[:]), COPY, scale=sb_t[:, t : t + 1])
+            nc.vector.tensor_tensor(larger[t][:], first[:], second[:], ALU.max)
 
-        for t in range(3):
-            put(t)
-        join(0)
-        put(3)
-        for t in range(1, PACK):
-            join(t)
+        def take_off(t):
+            third = sbuf(f"third{t}", [P, O], F32)
+            nc.scalar.activation(third[:], b_rows[t][:].indirect(list6[:]), COPY, scale=sd_t[:, t : t + 1])
+            nc.vector.tensor_tensor(hid[:, :, t], larger[t][:], third[:], ALU.subtract)
+
+        put(0, 1)
+        for t in range(PACK):
+            if t + 1 < PACK:
+                put(t + 1, 1)
+            pick(t)
+            if t > 0:
+                take_off(t - 1)
+        take_off(PACK - 1)
 
         hid_w = sbuf("hid_w", [P, O], U32)
         hid_s = sbuf("hid_s", [P, O], U8)

@@ -49,11 +49,11 @@ def tile_list_ownthree_noted_one_ownpage_kernel(
             queue.dma_start(tile[:].bitcast(I32), rows.bitcast(I32))
             return tile
 
-        def load_scale_rows(stage, src, first):
+        def load_scale_rows(stage, base, src, first):
             words = src.shape[2] // 4
             rows = src[0].bitcast(I32).rearrange("(s q r) n -> q r s n", s=2, q=2)
             for q in range(2):
-                nc.sync.dma_start(stage[32 * q : 32 * q + 4, :, first : first + words], rows[q])
+                nc.sync.dma_start(stage[base + 32 * q : base + 32 * q + 4, :, first : first + words], rows[q])
 
         def load_factor(name, src):
             tile = sbuf(name, [P, PACK], F32)
@@ -67,27 +67,27 @@ def tile_list_ownthree_noted_one_ownpage_kernel(
             )
 
         xo_stage = sbuf("xo_stage", [64, 2, Z // 4], I32)
-        xt_stage = sbuf("xt_stage", [64, 2, T // 4], I32)
+        xt_stage = sbuf("xt_stage", [P, 2, T // 4], I32)
         a_stage = sbuf("a_stage", [P, 2, 2 * R // 4], I32)
         b_stage = sbuf("b_stage", [P, 2, (R + N) // 4], I32)
         nc.vector.memset(xo_stage[:], 0)
-        nc.vector.memset(xt_stage[:], 0)
+        nc.vector.memset(xt_stage[64:128], 0)
         nc.vector.memset(a_stage[0:64], 0)
-        nc.vector.memset(b_stage[0:64], 0)
+        nc.vector.memset(b_stage[64:128], 0)
 
         list2 = load_list("list2", offs2)
         xo_w = load_words("xo_w", xo_words, Z, U16)
-        load_scale_rows(xo_stage, xo_scales, 0)
-        load_scale_rows(xt_stage, xt_scales, 0)
+        load_scale_rows(xo_stage, 0, xo_scales, 0)
+        load_scale_rows(xt_stage, 64, xt_scales, 0)
         list1 = load_list("list1", offs)
         xt_w = load_words("xt_w", xt_words, T, U32)
-        load_scale_rows(a_stage, w0_scales, 0)
-        load_scale_rows(a_stage, w_scales, R // 4)
+        load_scale_rows(a_stage, 0, w0_scales, 0)
+        load_scale_rows(a_stage, 0, w_scales, R // 4)
         w0_w = load_words("w0_w", w0_words, R, U32, nc.gpsimd)
         w_w = load_words("w_w", w_words, R, U16, nc.gpsimd)
         list3 = load_list("list3", offs3)
-        load_scale_rows(b_stage, w2_scales, 0)
-        load_scale_rows(b_stage, wb_scales, R // 4)
+        load_scale_rows(b_stage, 64, w2_scales, 0)
+        load_scale_rows(b_stage, 64, wb_scales, R // 4)
         w2_w = load_words("w2_w", w2_words, R, I32)
         wb_w = load_words("wb_w", wb_words, N, U32)
         list7 = load_list("list7", offs7)
@@ -99,8 +99,8 @@ def tile_list_ownthree_noted_one_ownpage_kernel(
         sd_t = load_factor("sd_t", sd)
 
         boards = [sbuf(f"board{i}", [P, C], F32) for i in range(PACK)]
-        for i, tile in enumerate(boards):
-            (nc.vector if i < 2 else nc.gpsimd).memset(tile[:], 0.0)
+        for tile in boards:
+            nc.vector.memset(tile[:], 0.0)
 
         def spread(name, stage, columns):
             plane = sbuf(name, [P, columns], U8)
@@ -117,8 +117,8 @@ def tile_list_ownthree_noted_one_ownpage_kernel(
 
         H = J // 2
         xo_gw = [gather(sbuf("xo_gw0", [P, H], U16), xo_w, list2, 0)]
-        xo_plane = spread("xo_plane", xo_stage, Z)
-        xt_plane = spread("xt_plane", xt_stage, T)
+        xo_plane = spread("xo_plane", xo_stage[:], Z)
+        xt_plane = spread("xt_plane", xt_stage[64:128], T)
         xo_gs = [gather(sbuf("xo_gs0", [P, H], U8), xo_plane, list2, 0)]
         xt_gs = [gather(placed("xt_gs0", [P, H], U8, 512), xt_plane, list1, 0)]
         nc.vector.tensor_copy(a_stage[64:128, 0, :], a_stage[0:64, 1, :])
@@ -160,8 +160,8 @@ def tile_list_ownthree_noted_one_ownpage_kernel(
         for t in range(PACK):
             first_stage(t, 1)
 
-        nc.vector.tensor_copy(b_stage[64:128, 0, :], b_stage[0:64, 1, :])
-        b_plane = b_stage[:, 0, :].bitcast(U8)
+        nc.vector.tensor_copy(b_stage[0:64, 1, :], b_stage[64:128, 0, :])
+        b_plane = b_stage[:, 1, :].bitcast(U8)
         w2_s = sbuf("w2_s", [P, R], U8)
         nc.vector.tensor_copy(*dealt(w2_s[:], b_plane[:, 0:R], 16))
         w2_d = sbuf("w2_d", [P, R], I32)
@@ -178,10 +178,6 @@ def tile_list_ownthree_noted_one_ownpage_kernel(
             nc.vector.tensor_copy(b_t[:], b_banks[t // 2][:, t % 2].rearrange("p h j -> p (h j)"))
             b_rows.append(b_t)
 
-        pages = [sbuf(f"page{i}", [P, E], F32, tag=tag) for i, tag in enumerate(("xt_w", "xo_w"))]
-        for tile in pages:
-            nc.gpsimd.memset(tile[:], 0.0)
-
         hid = sbuf("hid", [P, O, PACK], BF16)
 
         larger = {}
@@ -194,10 +190,11 @@ def tile_list_ownthree_noted_one_ownpage_kernel(
             nc.scalar.activation(second[:], boards[t][:].indirect(list5[:]), COPY, scale=sb_t[:, t : t + 1])
             nc.vector.tensor_tensor(larger[t][:], first[:], second[:], ALU.max)
 
-        def take_off(t):
-            third = sbuf(f"third{t}", [P, O], F32)
-            nc.scalar.activation(third[:], b_rows[t][:].indirect(list6[:]), COPY, scale=sd_t[:, t : t + 1])
-            nc.vector.tensor_tensor(hid[:, :, t], larger[t][:], third[:], ALU.subtract)
+        def take_off(t, places):
+            third = sbuf(f"third{t}_{places.start}", [P, places.stop - places.start], F32)
+            offsets = list6[:, places.start // 16 : places.stop // 16]
+            nc.scalar.activation(third[:], b_rows[t][:].indirect(offsets), COPY, scale=sd_t[:, t : t + 1])
+            nc.vector.tensor_tensor(hid[:, places, t], larger[t][:, places], third[:], ALU.subtract)
 
         put(0, 1)
         for t in range(PACK):
@@ -205,12 +202,20 @@ def tile_list_ownthree_noted_one_ownpage_kernel(
                 put(t + 1, 1)
             pick(t)
             if t > 0:
-                take_off(t - 1)
-        take_off(PACK - 1)
+                take_off(t - 1, slice(0, O))
+
+        pages = [sbuf(f"page{i}", [P, E], F32, tag=tag) for i, tag in enumerate(("w2_w", "board0"))]
+        for tile in pages:
+            nc.gpsimd.memset(tile[:], 0.0)
 
         hid_w = sbuf("hid_w", [P, O], U32)
         hid_s = sbuf("hid_s", [P, O], U8)
-        nc.vector.quantize_mx(out=hid_w[:].bitcast(E4M3), scales=hid_s[:], in_=hid[:].rearrange("p o t -> p (o t)"))
+        halves = (slice(0, O // 2), slice(O // 2, O))
+        for places in halves:
+            take_off(PACK - 1, places)
+        for places in halves:
+            nc.vector.quantize_mx(out=hid_w[:, places].bitcast(E4M3), scales=hid_s[:, places],
+                                  in_=hid[:, places, :].rearrange("p o t -> p (o t)"))
 
         for i in range(N // P):
             p_bank = psum.tile([P, O], F32, name=f"p_bank{i}")

@@ -67,27 +67,34 @@ def tile_list_ownthree_noted_one_ownpage_kernel(
             )
 
         xo_stage = sbuf("xo_stage", [64, 2, Z // 4], I32)
-        xt_stage = sbuf("xt_stage", [P, 2, T // 4], I32)
+        xt_plane = sbuf("xt_plane", [P, T], U8)
         a_stage = sbuf("a_stage", [P, 2, 2 * R // 4], I32)
         b_stage = sbuf("b_stage", [P, 2, (R + N) // 4], I32)
         nc.vector.memset(xo_stage[:], 0)
-        nc.vector.memset(xt_stage[64:128], 0)
-        nc.vector.memset(a_stage[0:64], 0)
-        nc.vector.memset(b_stage[64:128], 0)
+        nc.vector.memset(xt_plane[:].bitcast(I32), 0)
+        nc.vector.memset(a_stage[64:128], 0)
+        nc.vector.memset(b_stage[0:64], 0)
 
+        def load_xt_quadrant(q):
+            rows = xt_scales[0].bitcast(I32)[4 * q : 4 * q + 4, :]
+            nc.sync.dma_start(xt_plane[32 * q : 32 * q + 4, :].bitcast(I32), rows)
+
+        w_w = load_words("w_w", w_words, R, U16, nc.gpsimd)
         list2 = load_list("list2", offs2)
         xo_w = load_words("xo_w", xo_words, Z, U16)
-        load_scale_rows(xo_stage, 0, xo_scales, 0)
-        load_scale_rows(xt_stage, 64, xt_scales, 0)
         list1 = load_list("list1", offs)
+        load_scale_rows(xo_stage, 0, xo_scales, 0)
+        load_xt_quadrant(2)
+        load_xt_quadrant(3)
         xt_w = load_words("xt_w", xt_words, T, U32)
-        load_scale_rows(a_stage, 0, w0_scales, 0)
-        load_scale_rows(a_stage, 0, w_scales, R // 4)
-        w0_w = load_words("w0_w", w0_words, R, U32, nc.gpsimd)
-        w_w = load_words("w_w", w_words, R, U16, nc.gpsimd)
+        load_xt_quadrant(0)
+        load_xt_quadrant(1)
+        load_scale_rows(a_stage, 64, w0_scales, 0)
+        load_scale_rows(a_stage, 64, w_scales, R // 4)
+        w0_w = load_words("w0_w", w0_words, R, U32)
         list3 = load_list("list3", offs3)
-        load_scale_rows(b_stage, 64, w2_scales, 0)
-        load_scale_rows(b_stage, 64, wb_scales, R // 4)
+        load_scale_rows(b_stage, 0, w2_scales, 0)
+        load_scale_rows(b_stage, 0, wb_scales, R // 4)
         w2_w = load_words("w2_w", w2_words, R, I32)
         wb_w = load_words("wb_w", wb_words, N, U32)
         list7 = load_list("list7", offs7)
@@ -118,22 +125,34 @@ def tile_list_ownthree_noted_one_ownpage_kernel(
         H = J // 2
         xo_gw = [gather(sbuf("xo_gw0", [P, H], U16), xo_w, list2, 0)]
         xo_plane = spread("xo_plane", xo_stage[:], Z)
-        xt_plane = spread("xt_plane", xt_stage[64:128], T)
         xo_gs = [gather(sbuf("xo_gs0", [P, H], U8), xo_plane, list2, 0)]
-        xt_gs = [gather(placed("xt_gs0", [P, H], U8, 512), xt_plane, list1, 0)]
-        nc.vector.tensor_copy(a_stage[64:128, 0, :], a_stage[0:64, 1, :])
         xt_gw = [gather(placed("xt_gw0", [P, H], U32, 0), xt_w, list1, 0)]
-        a_plane = a_stage[:, 0, :].bitcast(U8).rearrange("p (w m t) -> p t w m", w=2, t=PACK)
+        xt_gs = [gather(placed("xt_gs0", [P, H], U8, 512), xt_plane, list1, 0)]
+        nc.vector.tensor_copy(a_stage[0:64, 1, :], a_stage[64:128, 0, :])
 
-        w0_dealt = sbuf("w0_dealt", [P, R], U32)
+        a_plane = a_stage[:, 1, :].bitcast(U8)
+        s_first = sbuf("s_first", [P, 2, P], U8)
+        s_rest = sbuf("s_rest", [P, 3, 2, P], U8)
+        nc.vector.tensor_copy(s_first[:], a_plane.rearrange("p (w m t) -> p t w m", w=2, t=PACK)[:, 0])
+        nc.vector.tensor_copy(
+            s_rest[:].rearrange("p t w (c i) -> p (w c) t i", i=16),
+            a_plane.rearrange("p (g i t) -> p g t i", t=PACK, i=16)[:, :, 1:PACK, :],
+        )
+        a_s = [s_first[:]] + [s_rest[:, t] for t in range(3)]
+
         w_dealt = sbuf("w_dealt", [P, R], U16)
-        nc.scalar.copy(*dealt(w0_dealt[:], w0_w[:], 4))
+        w0_first = sbuf("w0_first", [P, P], U32)
+        w0_rest = sbuf("w0_rest", [P, 3 * P], U32)
         nc.scalar.copy(*dealt(w_dealt[:], w_w[:], 8))
-        w0_d = [w0_dealt[:, P * t : P * (t + 1)] for t in range(PACK)]
+        nc.scalar.copy(w0_first[:], w0_w[:].rearrange("p (m t) -> p t m", t=PACK)[:, 0, :])
+        nc.scalar.copy(
+            w0_rest[:].rearrange("p (t c i) -> p c t i", t=3, i=4),
+            w0_w[:].rearrange("p (c i t) -> p c t i", t=PACK, i=4)[:, :, 1:PACK, :],
+        )
+        w0_d = [w0_first[:]] + [w0_rest[:, P * t : P * (t + 1)] for t in range(3)]
         w_d = [w_dealt[:, P * t : P * (t + 1)] for t in range(PACK)]
 
         a_banks = [psum.tile([P, 2, H], F32, name=f"a_bank{t}") for t in range(PACK)]
-        a_s = []
         a_rows = {}
 
         def first_stage(t, h):
@@ -142,26 +161,27 @@ def tile_list_ownthree_noted_one_ownpage_kernel(
             nc.tensor.matmul_mx(a_banks[t][:, h, :], lhsT=w_d[t].bitcast(E2M1), lhsT_scale=a_s[t][:, 1, :],
                                 rhs=xt_gw[h][:].bitcast(E4M3), rhs_scale=xt_gs[h][:], start=False, stop=True)
             a_rows[t, h] = sbuf(f"a_rows{t}{h}", [P, H], F32)
-            nc.vector.tensor_copy(a_rows[t, h][:], a_banks[t][:, h, :])
+            if (t, h) == (0, 0):
+                nc.scalar.copy(a_rows[t, h][:], a_banks[t][:, h, :])
+            else:
+                nc.vector.tensor_copy(a_rows[t, h][:], a_banks[t][:, h, :])
 
         def put(t, h):
             nc.scalar.activation(boards[t][:].indirect(half(list3, h)), a_rows[t, h][:], COPY)
 
         for t in range(PACK):
-            a_s.append(sbuf(f"a_s{t}", [P, 2, P], U8))
-            nc.vector.tensor_copy(a_s[t][:], a_plane[:, t])
             first_stage(t, 0)
             put(t, 0)
 
-        xo_gw.append(gather(placed("xo_gw1", [P, H], U16, 0), xo_w, list2, 1))
+        xo_gw.append(gather(sbuf("xo_gw1", [P, H], U16, tag="w0_w"), xo_w, list2, 1))
         xo_gs.append(gather(placed("xo_gs1", [P, H], U8, 256), xo_plane, list2, 1))
         xt_gs.append(gather(placed("xt_gs1", [P, H], U8, 384), xt_plane, list1, 1))
         xt_gw.append(gather(placed("xt_gw1", [P, H], U32, 512), xt_w, list1, 1))
         for t in range(PACK):
             first_stage(t, 1)
 
-        nc.vector.tensor_copy(b_stage[0:64, 1, :], b_stage[64:128, 0, :])
-        b_plane = b_stage[:, 1, :].bitcast(U8)
+        nc.vector.tensor_copy(b_stage[64:128, 0, :], b_stage[0:64, 1, :])
+        b_plane = b_stage[:, 0, :].bitcast(U8)
         w2_s = sbuf("w2_s", [P, R], U8)
         nc.vector.tensor_copy(*dealt(w2_s[:], b_plane[:, 0:R], 16))
         w2_d = sbuf("w2_d", [P, R], I32)
@@ -180,29 +200,37 @@ def tile_list_ownthree_noted_one_ownpage_kernel(
 
         hid = sbuf("hid", [P, O, PACK], BF16)
 
-        larger = {}
+        larger = [sbuf(f"larger{u}", [P, 2, O], F32, tag="w2_d" if u == 0 else None) for u in range(2)]
+        third = [sbuf(f"third{u}", [P, 2, O], F32) for u in range(2)]
 
         def pick(t):
             first = sbuf(f"first{t}", [P, O], F32)
             second = sbuf(f"second{t}", [P, O], F32)
-            larger[t] = sbuf(f"larger{t}", [P, O], F32, tag="w2_d" if t == 0 else None)
             nc.scalar.activation(first[:], boards[t][:].indirect(list4[:]), COPY, scale=sa_t[:, t : t + 1])
             nc.scalar.activation(second[:], boards[t][:].indirect(list5[:]), COPY, scale=sb_t[:, t : t + 1])
-            nc.vector.tensor_tensor(larger[t][:], first[:], second[:], ALU.max)
+            nc.vector.tensor_tensor(larger[t // 2][:, t % 2, :], first[:], second[:], ALU.max)
 
-        def take_off(t, places):
-            third = sbuf(f"third{t}_{places.start}", [P, places.stop - places.start], F32)
+        def take_off(u, places):
             offsets = list6[:, places.start // 16 : places.stop // 16]
-            nc.scalar.activation(third[:], b_rows[t][:].indirect(offsets), COPY, scale=sd_t[:, t : t + 1])
-            nc.vector.tensor_tensor(hid[:, places, t], larger[t][:, places], third[:], ALU.subtract)
+            for t in (2 * u, 2 * u + 1):
+                nc.scalar.activation(third[u][:, t % 2, places], b_rows[t][:].indirect(offsets), COPY,
+                                     scale=sd_t[:, t : t + 1])
+            nc.vector.tensor_tensor(
+                hid[:, places, 2 * u : 2 * u + 2],
+                larger[u][:, :, places].rearrange("p t o -> p o t"),
+                third[u][:, :, places].rearrange("p t o -> p o t"),
+                ALU.subtract,
+            )
 
         put(0, 1)
-        for t in range(PACK):
-            if t + 1 < PACK:
-                put(t + 1, 1)
-            pick(t)
-            if t > 0:
-                take_off(t - 1, slice(0, O))
+        put(1, 1)
+        pick(0)
+        put(2, 1)
+        pick(1)
+        put(3, 1)
+        take_off(0, slice(0, O))
+        pick(2)
+        pick(3)
 
         pages = [sbuf(f"page{i}", [P, E], F32, tag=tag) for i, tag in enumerate(("w2_w", "board0"))]
         for tile in pages:
@@ -212,7 +240,7 @@ def tile_list_ownthree_noted_one_ownpage_kernel(
         hid_s = sbuf("hid_s", [P, O], U8)
         halves = (slice(0, O // 2), slice(O // 2, O))
         for places in halves:
-            take_off(PACK - 1, places)
+            take_off(1, places)
         for places in halves:
             nc.vector.quantize_mx(out=hid_w[:, places].bitcast(E4M3), scales=hid_s[:, places],
                                   in_=hid[:, places, :].rearrange("p o t -> p (o t)"))

from contextlib import ExitStack

import concourse.mybir as mybir

F32 = mybir.dt.float32
BF16 = mybir.dt.bfloat16
I32 = mybir.dt.int32
U32 = mybir.dt.uint32
U16 = mybir.dt.uint16
U8 = mybir.dt.uint8
E4M3 = mybir.dt.float8_e4m3fn_x4
E5M2 = mybir.dt.float8_e5m2_x4
E2M1 = mybir.dt.float4_e2m1fn_x4
COPY = mybir.ActivationFunctionType.Copy
ALU = mybir.AluOpType

P = 128
PACK = 4
K, T, J, R, F, Z, C, O, N, E = 512, 1024, 256, 512, 512, 1024, 512, 128, 256, 512
FLOPS = 2 * (K * R * J + 2 * F * R * J + R * N * O)


def tile_list_ownthree_noted_one_ownpage_kernel(
    tc, xt_words, xt_scales, xo_words, xo_scales, w_words, w_scales, w0_words, w0_scales,
    w2_words, w2_scales, sa, sb, sd, wb_words, wb_scales,
    offs, offs2, offs3, offs4, offs5, offs6, offs7, out,
):
    nc = tc.nc
    with ExitStack() as ctx:
        keep = ctx.enter_context(tc.tile_pool(name="keep", bufs=1))
        psum = ctx.enter_context(tc.psum_pool(name="psum", bufs=1))

        reuse = ctx.enter_context(tc.tile_pool(name="reuse", bufs=1))

        def sbuf(name, shape, dtype, tag=None):
            return keep.tile(shape, dtype, name=name, tag=tag or name, align_bytes=64)

        def placed(name, shape, dtype, offset):
            return reuse.tile(shape, dtype, name=name, offset=offset, align_bytes=64)

        def load_list(name, src):
            tile = keep.tile(list(src.shape), U16, name=name)
            nc.sync.dma_start(tile[:], src)
            return tile

        def load_words(name, src, columns, dtype, queue=nc.sync):
            tile = sbuf(name, [P, columns], dtype)
            rows = src[0] if len(src.shape) == 3 else src[0].rearrange("p n t -> p (n t)")
            queue.dma_start(tile[:].bitcast(I32), rows.bitcast(I32))
            return tile

        def load_scale_rows(stage, base, src, first):
            words = src.shape[2] // 4
            rows = src[0].bitcast(I32).rearrange("(s q r) n -> q r s n", s=2, q=2)
            for q in range(2):
                nc.sync.dma_start(stage[base + 32 * q : base + 32 * q + 4, :, first : first + words], rows[q])

        def load_factor(name, src):
            tile = sbuf(name, [P, PACK], F32)
            nc.sync.dma_start(tile[:], src.rearrange("(p t) o -> p (t o)", t=PACK))
            return tile

        def dealt(dst, src, run):
            return (
                dst.rearrange("p (t c i) -> p c t i", t=PACK, i=run),
                src.rearrange("p (c i t) -> p c t i", t=PACK, i=run),
            )

        xo_stage = sbuf("xo_stage", [64, 2, Z // 4], I32)
        xt_plane = sbuf("xt_plane", [P, T], U8)
        a_stage = sbuf("a_stage", [P, 2, 2 * R // 4], I32)
        b_stage = sbuf("b_stage", [P, 2, (R + N) // 4], I32)
        nc.vector.memset(xo_stage[:], 0)
        nc.vector.memset(xt_plane[:].bitcast(I32), 0)
        nc.vector.memset(a_stage[64:128], 0)
        nc.vector.memset(b_stage[0:64], 0)

        def load_xt_quadrant(q):
            rows = xt_scales[0].bitcast(I32)[4 * q : 4 * q + 4, :]
            nc.sync.dma_start(xt_plane[32 * q : 32 * q + 4, :].bitcast(I32), rows)

        w_w = load_words("w_w", w_words, R, U16, nc.gpsimd)
        list2 = load_list("list2", offs2)
        xo_w = load_words("xo_w", xo_words, Z, U16)
        list1 = load_list("list1", offs)
        load_scale_rows(xo_stage, 0, xo_scales, 0)
        load_xt_quadrant(2)
        load_xt_quadrant(3)
        xt_w = load_words("xt_w", xt_words, T, U32)
        load_xt_quadrant(0)
        load_xt_quadrant(1)
        load_scale_rows(a_stage, 64, w0_scales, 0)
        load_scale_rows(a_stage, 64, w_scales, R // 4)
        w0_w = load_words("w0_w", w0_words, R, U32)
        list3 = load_list("list3", offs3)
        load_scale_rows(b_stage, 0, w2_scales, 0)
        load_scale_rows(b_stage, 0, wb_scales, R // 4)
        w2_w = load_words("w2_w", w2_words, R, I32)
        wb_w = load_words("wb_w", wb_words, N, U32)
        list7 = load_list("list7", offs7)
        list4 = load_list("list4", offs4)
        sa_t = load_factor("sa_t", sa)
        list5 = load_list("list5", offs5)
        sb_t = load_factor("sb_t", sb)
        list6 = load_list("list6", offs6)
        sd_t = load_factor("sd_t", sd)

        boards = [sbuf(f"board{i}", [P, C], F32) for i in range(PACK)]
        for tile in boards:
            nc.vector.memset(tile[:], 0.0)

        def spread(name, stage, columns):
            plane = sbuf(name, [P, columns], U8)
            for s in range(2):
                nc.vector.tensor_copy(plane[64 * s : 64 * s + 64, :].bitcast(I32), stage[:, s, :])
            return plane

        def half(offsets, h):
            return offsets[:, 8 * h : 8 * h + 8]

        def gather(picked, window, offsets, h):
            nc.vector.tensor_copy(picked[:], window[:].indirect(half(offsets, h)))
            return picked

        H = J // 2
        xo_gw = [gather(sbuf("xo_gw0", [P, H], U16), xo_w, list2, 0)]
        xo_plane = spread("xo_plane", xo_stage[:], Z)
        xo_gs = [gather(sbuf("xo_gs0", [P, H], U8), xo_plane, list2, 0)]
        xt_gw = [gather(placed("xt_gw0", [P, H], U32, 0), xt_w, list1, 0)]
        xt_gs = [gather(placed("xt_gs0", [P, H], U8, 512), xt_plane, list1, 0)]
        nc.vector.tensor_copy(a_stage[0:64, 1, :], a_stage[64:128, 0, :])

        a_plane = a_stage[:, 1, :].bitcast(U8)
        s_first = sbuf("s_first", [P, 2, P], U8)
        s_rest = sbuf("s_rest", [P, 3, 2, P], U8)
        nc.vector.tensor_copy(s_first[:], a_plane.rearrange("p (w m t) -> p t w m", w=2, t=PACK)[:, 0])
        nc.vector.tensor_copy(
            s_rest[:].rearrange("p t w (c i) -> p (w c) t i", i=16),
            a_plane.rearrange("p (g i t) -> p g t i", t=PACK, i=16)[:, :, 1:PACK, :],
        )
        a_s = [s_first[:]] + [s_rest[:, t] for t in range(3)]

        w_dealt = sbuf("w_dealt", [P, R], U16)
        w0_first = sbuf("w0_first", [P, P], U32)
        w0_rest = sbuf("w0_rest", [P, 3 * P], U32)
        nc.scalar.copy(*dealt(w_dealt[:], w_w[:], 8))
        nc.scalar.copy(w0_first[:], w0_w[:].rearrange("p (m t) -> p t m", t=PACK)[:, 0, :])
        nc.scalar.copy(
            w0_rest[:].rearrange("p (t c i) -> p c t i", t=3, i=4),
            w0_w[:].rearrange("p (c i t) -> p c t i", t=PACK, i=4)[:, :, 1:PACK, :],
        )
        w0_d = [w0_first[:]] + [w0_rest[:, P * t : P * (t + 1)] for t in range(3)]
        w_d = [w_dealt[:, P * t : P * (t + 1)] for t in range(PACK)]

        a_banks = [psum.tile([P, 2, H], F32, name=f"a_bank{t}") for t in range(PACK)]
        a_rows = {}

        def first_stage(t, h):
            nc.tensor.matmul_mx(a_banks[t][:, h, :], lhsT=w0_d[t].bitcast(E5M2), lhsT_scale=a_s[t][:, 0, :],
                                rhs=xo_gw[h][:].bitcast(E2M1), rhs_scale=xo_gs[h][:], start=True, stop=False)
            nc.tensor.matmul_mx(a_banks[t][:, h, :], lhsT=w_d[t].bitcast(E2M1), lhsT_scale=a_s[t][:, 1, :],
                                rhs=xt_gw[h][:].bitcast(E4M3), rhs_scale=xt_gs[h][:], start=False, stop=True)
            a_rows[t, h] = sbuf(f"a_rows{t}{h}", [P, H], F32)
            if (t, h) == (0, 0):
                nc.scalar.copy(a_rows[t, h][:], a_banks[t][:, h, :])
            else:
                nc.vector.tensor_copy(a_rows[t, h][:], a_banks[t][:, h, :])

        def put(t, h):
            nc.scalar.activation(boards[t][:].indirect(half(list3, h)), a_rows[t, h][:], COPY)

        for t in range(PACK):
            first_stage(t, 0)
            put(t, 0)

        xo_gw.append(gather(sbuf("xo_gw1", [P, H], U16, tag="w0_w"), xo_w, list2, 1))
        xo_gs.append(gather(placed("xo_gs1", [P, H], U8, 256), xo_plane, list2, 1))
        xt_gs.append(gather(placed("xt_gs1", [P, H], U8, 384), xt_plane, list1, 1))
        xt_gw.append(gather(placed("xt_gw1", [P, H], U32, 512), xt_w, list1, 1))
        for t in range(PACK):
            first_stage(t, 1)

        nc.vector.tensor_copy(b_stage[64:128, 0, :], b_stage[0:64, 1, :])
        b_plane = b_stage[:, 0, :].bitcast(U8)
        w2_s = sbuf("w2_s", [P, R], U8)
        nc.vector.tensor_copy(*dealt(w2_s[:], b_plane[:, 0:R], 16))
        w2_d = sbuf("w2_d", [P, R], I32)
        nc.vector.tensor_copy(*dealt(w2_d[:], w2_w[:], 4))
        b_banks = [psum.tile([P, 2, 2, H], F32, name=f"b_bank{i}") for i in range(2)]
        b_rows = []
        for t in range(PACK):
            cols = slice(P * t, P * (t + 1))
            for h in range(2):
                nc.tensor.matmul_mx(b_banks[t // 2][:, t % 2, h, :], lhsT=w2_d[:, cols].bitcast(E5M2), lhsT_scale=w2_s[:, cols],
                                    rhs=xo_gw[h][:].bitcast(E2M1), rhs_scale=xo_gs[h][:], start=True, stop=True)
        for t in range(PACK):
            b_t = sbuf(f"b_rows{t}", [P, J], F32)
            nc.vector.tensor_copy(b_t[:], b_banks[t // 2][:, t % 2].rearrange("p h j -> p (h j)"))
            b_rows.append(b_t)

        hid = sbuf("hid", [P, O, PACK], BF16)

        larger = [sbuf(f"larger{u}", [P, 2, O], F32, tag="w2_d" if u == 0 else None) for u in range(2)]
        third = [sbuf(f"third{u}", [P, 2, O], F32) for u in range(2)]

        def pick(t):
            first = sbuf(f"first{t}", [P, O], F32)
            second = sbuf(f"second{t}", [P, O], F32)
            nc.scalar.activation(first[:], boards[t][:].indirect(list4[:]), COPY, scale=sa_t[:, t : t + 1])
            nc.scalar.activation(second[:], boards[t][:].indirect(list5[:]), COPY, scale=sb_t[:, t : t + 1])
            nc.vector.tensor_tensor(larger[t // 2][:, t % 2, :], first[:], second[:], ALU.max)

        def take_off(u, places):
            offsets = list6[:, places.start // 16 : places.stop // 16]
            for t in (2 * u, 2 * u + 1):
                nc.scalar.activation(third[u][:, t % 2, places], b_rows[t][:].indirect(offsets), COPY,
                                     scale=sd_t[:, t : t + 1])
            nc.vector.tensor_tensor(
                hid[:, places, 2 * u : 2 * u + 2],
                larger[u][:, :, places].rearrange("p t o -> p o t"),
                third[u][:, :, places].rearrange("p t o -> p o t"),
                ALU.subtract,
            )

        put(0, 1)
        put(1, 1)
        pick(0)
        put(2, 1)
        pick(1)
        put(3, 1)
        take_off(0, slice(0, O))
        pick(2)
        pick(3)

        pages = [sbuf(f"page{i}", [P, E], F32, tag=tag) for i, tag in enumerate(("w2_w", "board0"))]
        for tile in pages:
            nc.gpsimd.memset(tile[:], 0.0)

        hid_w = sbuf("hid_w", [P, O], U32)
        hid_s = sbuf("hid_s", [P, O], U8)
        halves = (slice(0, O // 2), slice(O // 2, O))
        for places in halves:
            take_off(1, places)
        for places in halves:
            nc.vector.quantize_mx(out=hid_w[:, places].bitcast(E4M3), scales=hid_s[:, places],
                                  in_=hid[:, places, :].rearrange("p o t -> p (o t)"))

        for i in range(N // P):
            p_bank = psum.tile([P, O], F32, name=f"p_bank{i}")
            nc.tensor.matmul_mx(p_bank[:], lhsT=wb_w[:, P * i : P * (i + 1)].bitcast(E5M2),
                                lhsT_scale=b_plane[:, R + P * i : R + P * (i + 1)],
                                rhs=hid_w[:].bitcast(E4M3), rhs_scale=hid_s[:], start=True, stop=True)
            p_rows = sbuf(f"p_rows{i}", [P, O], F32)
            nc.vector.tensor_copy(p_rows[:], p_bank[:])
            nc.scalar.activation(pages[i][:].indirect(list7[:]), p_rows[:], COPY)
            nc.sync.dma_start(out[P * i : P * (i + 1), :], pages[i][:])
